import numpy as np
import ml_dtypes


def mxq(x, axis, fmt="e4m3"):
    dtype, down = {"e4m3": (ml_dtypes.float8_e4m3fn, 7), "e5m2": (ml_dtypes.float8_e5m2, 14)}[fmt]
    v = np.moveaxis(np.asarray(x, np.float32).astype(ml_dtypes.bfloat16).astype(np.float64), axis, -1)
    blocks = v.reshape(v.shape[:-1] + (-1, 32))
    amax = np.abs(blocks).max(-1, keepdims=True)
    byte = np.maximum(np.where(amax > 0, np.frexp(amax)[1] - 1 + 127, 0) - down, 1)
    scale = np.exp2(byte - 127.0)
    codes = (blocks / scale).astype(np.float32).astype(dtype).astype(np.float64)
    return np.moveaxis((codes * scale).reshape(v.shape), -1, axis)


WIDE = False


def mx_kscale(k):
    if not WIDE:
        return np.ones(k)
    levels = np.array([30, -30])
    if k % 512:
        return np.exp2(np.random.permutation(np.resize(levels, k // 32))).repeat(32)
    a = np.empty((k // 512, 16))
    for p in range(k // 512):
        a[p, :8] = np.random.permutation(np.resize(levels, 8))
        for g in range(8):
            far = levels[np.abs(levels - a[p, g]) >= 10]
            a[p, g + 8] = far[np.random.randint(len(far))]
    return np.exp2(a.ravel()).repeat(32)


def f64(x):
    return np.asarray(x).astype(np.float64)


def striped(idx):
    return np.tile(np.asarray(idx).reshape(-1, 16).T, (8, 1)).astype(np.uint16)


def unstriped(offs):
    return offs[:16].T.reshape(-1).astype(np.int64)


E2M1 = np.array([0.0, 0.5, 1.0, 1.5, 2.0, 3.0, 4.0, 6.0, -0.0, -0.5, -1.0, -1.5, -2.0, -3.0, -4.0, -6.0])


def pack_weight(w, fmt):
    k, n = w.shape
    w = f64(np.asarray(w, np.float32).astype(ml_dtypes.bfloat16)).reshape(k // 32, 32, n)
    amax = np.abs(w).max(1)
    if fmt == "e4m3":
        byte = np.frexp(amax)[1] - 1 + 127 - 7
    else:
        mant, ex = np.frexp(amax / 6.0)
        byte = np.where(mant > 0.5, ex, ex - 1) + 127
    byte = np.clip(np.where(amax > 0, byte, 1), 1, 254)
    scaled = (w * np.exp2(127.0 - byte)[:, None, :]).reshape(k, n).astype(np.float32)
    by_word = np.ascontiguousarray(scaled.reshape(k // 512, 128, 4, n).transpose(0, 1, 3, 2))
    if fmt == "e4m3":
        words = by_word.astype(ml_dtypes.float8_e4m3fn).view(np.uint8)
    else:
        c = by_word.astype(ml_dtypes.float4_e2m1fn).view(np.uint8) & 0xF
        words = (c[..., 0::2] | (c[..., 1::2] << 4)).reshape(k // 512, 128, 2 * n)
    return np.ascontiguousarray(words), np.ascontiguousarray(byte.astype(np.uint8).reshape(k // 512, 16, n))


def unpack_weight(words, scales, fmt):
    g, _, n = scales.shape
    words = np.ascontiguousarray(words).reshape(g, 128, n, -1)
    if fmt == "e4m3":
        vals = words.view(ml_dtypes.float8_e4m3fn).astype(np.float64)
    else:
        nib = np.empty((g, 128, n, 4), np.uint8)
        nib[..., 0::2] = words & 0xF
        nib[..., 1::2] = words >> 4
        vals = E2M1[nib]
    vals = vals * np.repeat(np.exp2(scales.astype(np.float64) - 127.0), 8, axis=1)[..., None]
    return vals.transpose(0, 1, 3, 2).reshape(g * 512, n)


K, T, Z, J, R, C, O, Q, N = 512, 1024, 1024, 256, 512, 512, 256, 1024, 256


def setup_inputs():
    n = np.random.standard_normal
    idx = np.random.permutation(T)[:J]
    idx2 = np.random.permutation(Z)[:J]
    idx3 = np.random.permutation(C)[:J]
    idx4 = np.random.permutation(C)[:O]
    idx5 = np.random.permutation(J)[:O]
    idx6 = np.random.permutation(Q)[:O]
    idx7 = np.random.permutation(T)[:O]
    fk = mx_kscale(K)
    fr = mx_kscale(R)
    xtp = pack_weight(n((K, T)) / fk[:, None], "e2m1")
    xop = pack_weight(n((K, Z)) / fk[:, None], "e4m3")
    wp = pack_weight(n((K, R)) * 1 / np.sqrt(K) * fk[:, None] * fr, "e4m3")
    wbp = pack_weight(n((R, N)) * 1 / np.sqrt(R) / fr[:, None], "e2m1")
    wsp = pack_weight(n((K, N)) * 1 / np.sqrt(K) * fk[:, None], "e4m3")
    return {
        "xt_words": xtp[0],
        "xt_scales": xtp[1],
        "xo_words": xop[0],
        "xo_scales": xop[1],
        "w_words": wp[0],
        "w_scales": wp[1],
        "ta": (np.random.uniform(-2.0, 1.0, (R, Q))).astype(np.float32),
        "wb_words": wbp[0],
        "wb_scales": wbp[1],
        "ws_words": wsp[0],
        "ws_scales": wsp[1],
        "offs": striped(idx),
        "offs2": striped(idx2),
        "offs3": striped(idx3),
        "offs4": striped(idx4),
        "offs5": striped(idx5),
        "offs6": striped(idx6),
        "offs7": striped(idx7),
    }


def reference(xt_words, xt_scales, xo_words, xo_scales, w_words, w_scales, ta, wb_words, wb_scales, ws_words, ws_scales, offs, offs2, offs3, offs4, offs5, offs6, offs7):
    idx = unstriped(offs)
    idx2 = unstriped(offs2)
    idx3 = unstriped(offs3)
    idx4 = unstriped(offs4)
    idx5 = unstriped(offs5)
    idx6 = unstriped(offs6)
    idx7 = unstriped(offs7)
    xtu = unpack_weight(xt_words, xt_scales, "e2m1")
    xou = unpack_weight(xo_words, xo_scales, "e4m3")
    wu = unpack_weight(w_words, w_scales, "e4m3")
    wbu = unpack_weight(wb_words, wb_scales, "e2m1")
    wsu = unpack_weight(ws_words, ws_scales, "e4m3")
    xtidxg = xtu[:, idx]
    a = wu.T @ xtidxg
    xoidx2g = xou[:, idx2]
    b = wu.T @ xoidx2g
    pw = np.zeros((R, C))
    pw[:, idx3] = a
    nm = -np.max(f64(ta), axis=1, keepdims=True)
    hid = np.abs(pw[:, idx4] - b[:, idx5]) * np.exp(f64(ta)[:, idx6] + nm)
    hidq = mxq(hid, 0, "e5m2")
    xtidx7g = xtu[:, idx7]
    y = wbu.T @ hidq + wsu.T @ xtidx7g
    return y

@@ -1,0 +1,198 @@
+from contextlib import ExitStack
+
+import concourse.mybir as mybir
+
+K, T, Z, J, R, C, O, Q, N = 512, 1024, 1024, 256, 512, 512, 256, 1024, 256
+FLOPS = 2 * (2 * K * R * J + R * N * O + K * N * O)
+
+F32 = mybir.dt.float32
+BF16 = mybir.dt.bfloat16
+I32 = mybir.dt.int32
+U32 = mybir.dt.uint32
+U16 = mybir.dt.uint16
+U8 = mybir.dt.uint8
+E4M3 = mybir.dt.float8_e4m3fn_x4
+E5M2 = mybir.dt.float8_e5m2_x4
+E2M1 = mybir.dt.float4_e2m1fn_x4
+ALU = mybir.AluOpType
+ACT = mybir.ActivationFunctionType
+AX = mybir.AxisListType
+P = 128
+PACK = 4
+
+
+def tile_list_fadedread_oneforboth_further_plain_kernel(
+    tc, xt_words, xt_scales, xo_words, xo_scales, w_words, w_scales, ta, wb_words, wb_scales,
+    ws_words, ws_scales, offs, offs2, offs3, offs4, offs5, offs6, offs7, out,
+):
+    nc = tc.nc
+    with ExitStack() as ctx:
+        lists = ctx.enter_context(tc.tile_pool(name="lists", bufs=1))
+        sb = ctx.enter_context(tc.tile_pool(name="sb", bufs=1))
+        ps = ctx.enter_context(tc.psum_pool(name="ps", bufs=1))
+
+        def new(name, shape, dtype):
+            return sb.tile(shape, dtype, name=name, align_bytes=64)
+
+        def load_list(name, src):
+            tile = lists.tile([P, J // 16], U16, name=name)
+            nc.sync.dma_start(tile[:], src)
+            return tile
+
+        def zeroed_plane(name, width):
+            tile = new(name, [P, width], U8)
+            nc.vector.memset(tile[:].bitcast(I32), 0)
+            return tile
+
+        def load_plane(queue, tile, src):
+            for quad in range(4):
+                queue.dma_start(out=tile[32 * quad : 32 * quad + 4, :].bitcast(I32),
+                                in_=src[0, 4 * quad : 4 * quad + 4, :].bitcast(I32))
+
+        def load_words(queue, name, src, width, dtype):
+            tile = new(name, [P, width], dtype)
+            queue.dma_start(out=tile[:].bitcast(I32), in_=src.bitcast(I32))
+            return tile
+
+        def gather(name, window, offsets, dtype):
+            tile = new(name, [P, J], dtype)
+            nc.vector.tensor_copy(tile[:], window[:].indirect(offsets[:]))
+            return tile
+
+        xt_s = zeroed_plane("xt_s", T)
+        w_s = zeroed_plane("w_s", R)
+        xo_s = zeroed_plane("xo_s", Z)
+        ws_s = zeroed_plane("ws_s", N)
+        wb_s = zeroed_plane("wb_s", N)
+        board = [new("board%d" % t, [P, C], F32) for t in range(PACK)]
+        for t in range(PACK):
+            nc.vector.memset(board[t][:], 0.0)
+
+        ta_rows = ta.rearrange("(p t) q -> t p q", t=PACK)
+        levels = [new("levels%d" % t, [P, Q], F32) for t in range(PACK)]
+        xt_w = load_words(nc.scalar, "xt_w", xt_words[0], T, U16)
+        l1 = load_list("l1", offs)
+        load_plane(nc.sync, xt_s, xt_scales)
+        w_w = load_words(nc.sync, "w_w", w_words[0].rearrange("p c r -> p (c r)"), R, U32)
+        xo_w = load_words(nc.sync, "xo_w", xo_words[0].rearrange("p c r -> p (c r)"), Z, U32)
+        load_plane(nc.sync, w_s, w_scales)
+        l7 = load_list("l7", offs7)
+        l2 = load_list("l2", offs2)
+        nc.sync.dma_start(out=levels[0][:], in_=ta_rows[0])
+        l3 = load_list("l3", offs3)
+        l6 = load_list("l6", offs6)
+        load_plane(nc.sync, xo_s, xo_scales)
+        nc.sync.dma_start(out=levels[1][:], in_=ta_rows[1])
+        nc.sync.dma_start(out=levels[2][:], in_=ta_rows[2])
+        l5 = load_list("l5", offs5)
+        nc.sync.dma_start(out=levels[3][:], in_=ta_rows[3])
+        l4 = load_list("l4", offs4)
+        ws_w = load_words(nc.sync, "ws_w", ws_words[0].rearrange("p c r -> p (c r)"), N, U32)
+        wb_w = load_words(nc.sync, "wb_w", wb_words[0], N, U16)
+        load_plane(nc.sync, ws_s, ws_scales)
+        load_plane(nc.sync, wb_s, wb_scales)
+
+        xa_w = gather("xa_w", xt_w, l1, U16)
+        xa_s = gather("xa_s", xt_s, l1, U8)
+        wp_w = new("wp_w", [P, R], U32)
+        wp_s = new("wp_s", [P, R], U8)
+        nc.vector.tensor_copy(wp_w[:].rearrange("p (t m) -> p m t", t=PACK), w_w[:].rearrange("p (m t) -> p m t", t=PACK))
+        nc.vector.tensor_copy(wp_s[:].rearrange("p (t m) -> p t m", t=PACK), w_s[:].rearrange("p (m t) -> p t m", t=PACK))
+
+        both = [new("both%d" % t, [P, 2 * J], F32) for t in range(PACK)]
+        early = 2
+        a_ps, b_ps, ab_ps = [], [], []
+        for t in range(PACK):
+            if t < early:
+                a_ps.append(ps.tile([P, J], F32, name="a_ps%d" % t)[:])
+                b_ps.append(ps.tile([P, J], F32, name="b_ps%d" % t)[:])
+                ab_ps.append(None)
+            else:
+                bank = ps.tile([P, 2 * J], F32, name="ab_ps%d" % t)
+                a_ps.append(bank[:, J:])
+                b_ps.append(bank[:, :J])
+                ab_ps.append(bank[:])
+        for t in range(PACK):
+            cols = slice(t * P, (t + 1) * P)
+            nc.tensor.matmul_mx(out=a_ps[t], lhsT=wp_w[:, cols].bitcast(E4M3), lhsT_scale=wp_s[:, cols],
+                                rhs=xa_w[:].bitcast(E2M1), rhs_scale=xa_s[:], start=True, stop=True)
+
+        neg_top = [new("neg_top%d" % t, [P, 1], F32) for t in range(PACK)]
+        fade = [new("fade%d" % t, [P, O], F32) for t in range(PACK)]
+        b_pick = [new("b_pick%d" % t, [P, O], F32) for t in range(PACK)]
+        diff = [new("diff%d" % t, [P, O], F32) for t in range(PACK)]
+        signed = new("signed", [P, PACK, O], F32)
+
+        xs_w = gather("xs_w", xt_w, l7, U16)
+        xs_s = gather("xs_s", xt_s, l7, U8)
+        xb_w = gather("xb_w", xo_w, l2, U32)
+        xb_s = gather("xb_s", xo_s, l2, U8)
+        for t in range(PACK):
+            cols = slice(t * P, (t + 1) * P)
+            nc.tensor.matmul_mx(out=b_ps[t], lhsT=wp_w[:, cols].bitcast(E4M3), lhsT_scale=wp_s[:, cols],
+                                rhs=xb_w[:].bitcast(E4M3), rhs_scale=xb_s[:], start=True, stop=True)
+        for t in range(PACK):
+            nc.vector.tensor_reduce(neg_top[t][:], levels[t][:], axis=AX.X, op=ALU.max, negate=True)
+
+        def put(t):
+            nc.scalar.activation(board[t][:].indirect(l3[:]), both[t][:, J:], ACT.Copy)
+
+        def look(t):
+            nc.scalar.activation(fade[t][:], levels[t][:].indirect(l6[:]), ACT.Exp, bias=neg_top[t][:])
+
+        for t in range(early):
+            nc.scalar.copy(both[t][:, J:], a_ps[t])
+            put(t)
+        look(0)
+        for t in range(early):
+            nc.scalar.copy(both[t][:, :J], b_ps[t])
+        for t in range(early, PACK):
+            nc.scalar.copy(both[t][:], ab_ps[t])
+        for t in range(early, PACK):
+            put(t)
+        nc.scalar.activation(b_pick[3][:], both[3][:].indirect(l5[:]), ACT.Copy)
+        for t in range(1, PACK):
+            look(t)
+
+        def pick(t):
+            nc.vector.tensor_copy(b_pick[t][:], both[t][:].indirect(l5[:]))
+
+        def subtract(t):
+            nc.vector.tensor_tensor(diff[t][:], board[t][:].indirect(l4[:]), b_pick[t][:], ALU.subtract)
+
+        def weigh(t):
+            nc.vector.tensor_tensor(signed[:, t, :], diff[t][:], fade[t][:], ALU.mult)
+
+        for t in range(3):
+            pick(t)
+        for t in range(PACK):
+            subtract(t)
+            if t > 0:
+                weigh(t - 1)
+        weigh(3)
+
+        y_ps = [ps.tile([P, O], F32, name="y_ps%d" % h) for h in range(2)]
+        for h in range(2):
+            cols = slice(h * P, (h + 1) * P)
+            nc.tensor.matmul_mx(out=y_ps[h][:], lhsT=ws_w[:, cols].bitcast(E4M3), lhsT_scale=ws_s[:, cols],
+                                rhs=xs_w[:].bitcast(E2M1), rhs_scale=xs_s[:], start=True, stop=False)
+
+        hid = new("hid", [P, PACK * O], BF16)
+        half = O // 2
+        nc.scalar.activation(hid[:, : PACK * half].rearrange("p (c i t) -> p c t i", i=4, t=PACK),
+                             signed[:, :, :half].rearrange("p t (c i) -> p c t i", i=4), ACT.Abs)
+        upper = signed[:, :, half:].rearrange("p t o -> p o t")
+        nc.vector.scalar_tensor_tensor(hid[:, PACK * half :].rearrange("p (o t) -> p o t", t=PACK),
+                                       upper, -1.0, upper, ALU.mult, ALU.max)
+        hid_w = new("hid_w", [P, O], U32)
+        hid_s = new("hid_s", [P, O], U8)
+        nc.vector.quantize_mx(out=hid_w[:].bitcast(E5M2), scales=hid_s[:], in_=hid[:])
+        y = [new("y%d" % h, [P, O], F32) for h in range(2)]
+        for h in range(2):
+            cols = slice(h * P, (h + 1) * P)
+            nc.tensor.matmul_mx(out=y_ps[h][:], lhsT=wb_w[:, cols].bitcast(E2M1), lhsT_scale=wb_s[:, cols],
+                                rhs=hid_w[:].bitcast(E5M2), rhs_scale=hid_s[:], start=False, stop=True)
+        nc.scalar.copy(y[0][:], y_ps[0][:])
+        nc.scalar.dma_start(out=out[0:P, :], in_=y[0][:])
+        nc.vector.tensor_copy(y[1][:], y_ps[1][:])
+        nc.sync.dma_start(out=out[P : 2 * P, :], in_=y[1][:])

@@ -104,7 +104,7 @@ def tile_list_fadedread_oneforboth_further_plain_kernel(
         a_ps, b_ps, ab_ps = [], [], []
         for t in range(PACK):
             if t < early:
-                a_ps.append(ps.tile([P, J], F32, name="a_ps%d" % t)[:])
+                a_ps.append(ps.tile([P, J], F32, name="a_ps%d" % t, tag="bank%d" % t)[:])
                 b_ps.append(ps.tile([P, J], F32, name="b_ps%d" % t)[:])
                 ab_ps.append(None)
             else:
@@ -117,11 +117,13 @@ def tile_list_fadedread_oneforboth_further_plain_kernel(
             nc.tensor.matmul_mx(out=a_ps[t], lhsT=wp_w[:, cols].bitcast(E4M3), lhsT_scale=wp_s[:, cols],
                                 rhs=xa_w[:].bitcast(E2M1), rhs_scale=xa_s[:], start=True, stop=True)
 
+        half = O // 2
         neg_top = [new("neg_top%d" % t, [P, 1], F32) for t in range(PACK)]
-        fade = [new("fade%d" % t, [P, O], F32) for t in range(PACK)]
+        fade = new("fade", [P, PACK, O], F32)
         b_pick = [new("b_pick%d" % t, [P, O], F32) for t in range(PACK)]
-        diff = [new("diff%d" % t, [P, O], F32) for t in range(PACK)]
-        signed = new("signed", [P, PACK, O], F32)
+        diff = new("diff", [P, PACK, O], F32)
+        size = new("size", [P, PACK, half], F32)
+        signed = new("signed", [P, PACK, half], F32)
 
         xs_w = gather("xs_w", xt_w, l7, U16)
         xs_s = gather("xs_s", xt_s, l7, U8)
@@ -131,15 +133,30 @@ def tile_list_fadedread_oneforboth_further_plain_kernel(
             cols = slice(t * P, (t + 1) * P)
             nc.tensor.matmul_mx(out=b_ps[t], lhsT=wp_w[:, cols].bitcast(E4M3), lhsT_scale=wp_s[:, cols],
                                 rhs=xb_w[:].bitcast(E4M3), rhs_scale=xb_s[:], start=True, stop=True)
-        for t in range(PACK):
+
+        def top(t):
             nc.vector.tensor_reduce(neg_top[t][:], levels[t][:], axis=AX.X, op=ALU.max, negate=True)
 
         def put(t):
             nc.scalar.activation(board[t][:].indirect(l3[:]), both[t][:, J:], ACT.Copy)
 
         def look(t):
-            nc.scalar.activation(fade[t][:], levels[t][:].indirect(l6[:]), ACT.Exp, bias=neg_top[t][:])
+            nc.scalar.activation(fade[:, t, :], levels[t][:].indirect(l6[:]), ACT.Exp, bias=neg_top[t][:])
 
+        def pick(t):
+            nc.vector.tensor_copy(b_pick[t][:], both[t][:].indirect(l5[:]))
+
+        def subtract(t):
+            nc.vector.tensor_tensor(diff[:, t, :], board[t][:].indirect(l4[:]), b_pick[t][:], ALU.subtract)
+
+        def magnitude(planes):
+            nc.scalar.activation(size[:, planes, :], diff[:, planes, :half], ACT.Abs)
+
+        def weigh(planes):
+            nc.vector.tensor_tensor(signed[:, planes, :], diff[:, planes, half:], fade[:, planes, half:], ALU.mult)
+
+        for t in range(PACK):
+            top(t)
         for t in range(early):
             nc.scalar.copy(both[t][:, J:], a_ps[t])
             put(t)
@@ -150,49 +167,52 @@ def tile_list_fadedread_oneforboth_further_plain_kernel(
             nc.scalar.copy(both[t][:], ab_ps[t])
         for t in range(early, PACK):
             put(t)
-        nc.scalar.activation(b_pick[3][:], both[3][:].indirect(l5[:]), ACT.Copy)
-        for t in range(1, PACK):
-            look(t)
-
-        def pick(t):
-            nc.vector.tensor_copy(b_pick[t][:], both[t][:].indirect(l5[:]))
-
-        def subtract(t):
-            nc.vector.tensor_tensor(diff[t][:], board[t][:].indirect(l4[:]), b_pick[t][:], ALU.subtract)
-
-        def weigh(t):
-            nc.vector.tensor_tensor(signed[:, t, :], diff[t][:], fade[t][:], ALU.mult)
-
-        for t in range(3):
-            pick(t)
         for t in range(PACK):
-            subtract(t)
-            if t > 0:
-                weigh(t - 1)
-        weigh(3)
+            pick(t)
+        look(1)
+        look(2)
+        subtract(0)
+        subtract(1)
+        magnitude(slice(0, 2))
+        look(3)
+        subtract(2)
+        subtract(3)
+        magnitude(slice(2, 4))
+        weigh(slice(0, 3))
+        weigh(slice(3, 4))
 
-        y_ps = [ps.tile([P, O], F32, name="y_ps%d" % h) for h in range(2)]
-        for h in range(2):
-            cols = slice(h * P, (h + 1) * P)
-            nc.tensor.matmul_mx(out=y_ps[h][:], lhsT=ws_w[:, cols].bitcast(E4M3), lhsT_scale=ws_s[:, cols],
-                                rhs=xs_w[:].bitcast(E2M1), rhs_scale=xs_s[:], start=True, stop=False)
+        y_lo = ps.tile([P, 2, half], F32, name="y_lo", tag="bank0")
+        y_hi = [ps.tile([P, half], F32, name="y_hi%d" % h) for h in range(2)]
+        y_ps = [[y_lo[:, 0, :], y_lo[:, 1, :]], [y_hi[0][:], y_hi[1][:]]]
+        for u in range(2):
+            places = slice(u * half, (u + 1) * half)
+            for h in range(2):
+                cols = slice(h * P, (h + 1) * P)
+                nc.tensor.matmul_mx(out=y_ps[u][h], lhsT=ws_w[:, cols].bitcast(E4M3), lhsT_scale=ws_s[:, cols],
+                                    rhs=xs_w[:, places].bitcast(E2M1), rhs_scale=xs_s[:, places],
+                                    start=(u == 1 or h == 0), stop=False)
 
-        hid = new("hid", [P, PACK * O], BF16)
-        half = O // 2
-        nc.scalar.activation(hid[:, : PACK * half].rearrange("p (c i t) -> p c t i", i=4, t=PACK),
-                             signed[:, :, :half].rearrange("p t (c i) -> p c t i", i=4), ACT.Abs)
-        upper = signed[:, :, half:].rearrange("p t o -> p o t")
-        nc.vector.scalar_tensor_tensor(hid[:, PACK * half :].rearrange("p (o t) -> p o t", t=PACK),
-                                       upper, -1.0, upper, ALU.mult, ALU.max)
-        hid_w = new("hid_w", [P, O], U32)
-        hid_s = new("hid_s", [P, O], U8)
-        nc.vector.quantize_mx(out=hid_w[:].bitcast(E5M2), scales=hid_s[:], in_=hid[:])
-        y = [new("y%d" % h, [P, O], F32) for h in range(2)]
-        for h in range(2):
-            cols = slice(h * P, (h + 1) * P)
-            nc.tensor.matmul_mx(out=y_ps[h][:], lhsT=wb_w[:, cols].bitcast(E2M1), lhsT_scale=wb_s[:, cols],
-                                rhs=hid_w[:].bitcast(E5M2), rhs_scale=hid_s[:], start=False, stop=True)
-        nc.scalar.copy(y[0][:], y_ps[0][:])
-        nc.scalar.dma_start(out=out[0:P, :], in_=y[0][:])
-        nc.vector.tensor_copy(y[1][:], y_ps[1][:])
-        nc.sync.dma_start(out=out[P : 2 * P, :], in_=y[1][:])
+        hid = [new("hid%d" % u, [P, PACK * half], BF16) for u in range(2)]
+        nc.vector.tensor_tensor(hid[0][:].rearrange("p (c i t) -> p c t i", i=4, t=PACK),
+                                size[:].rearrange("p t (c i) -> p c t i", i=4),
+                                fade[:, :, :half].rearrange("p t (c i) -> p c t i", i=4), ALU.mult)
+        nc.scalar.activation(hid[1][:].rearrange("p (c i t) -> p c t i", i=4, t=PACK),
+                             signed[:].rearrange("p t (c i) -> p c t i", i=4), ACT.Abs)
+        for u in range(2):
+            hid_w = new("hid_w%d" % u, [P, half], U32)
+            hid_s = new("hid_s%d" % u, [P, half], U8)
+            nc.vector.quantize_mx(out=hid_w[:].bitcast(E5M2), scales=hid_s[:], in_=hid[u][:])
+            for h in range(2):
+                cols = slice(h * P, (h + 1) * P)
+                nc.tensor.matmul_mx(out=y_ps[u][h], lhsT=wb_w[:, cols].bitcast(E2M1), lhsT_scale=wb_s[:, cols],
+                                    rhs=hid_w[:].bitcast(E5M2), rhs_scale=hid_s[:],
+                                    start=False, stop=(u == 1 or h == 1))
+        out_rows = out.rearrange("(h p) o -> p h o", h=2)
+        y_a = new("y_a", [P, 2, half], F32)
+        nc.vector.tensor_copy(y_a[:], y_lo[:])
+        nc.sync.dma_start(out=out_rows[:, :, :half], in_=y_a[:])
+        y_b = [new("y_b%d" % h, [P, half], F32) for h in range(2)]
+        nc.scalar.copy(y_b[0][:], y_hi[0][:])
+        nc.scalar.dma_start(out=out_rows[:, 0, half:], in_=y_b[0][:])
+        nc.vector.tensor_copy(y_b[1][:], y_hi[1][:])
+        nc.sync.dma_start(out=out_rows[:, 1, half:], in_=y_b[1][:])

@@ -83,10 +83,10 @@ def tile_list_fadedread_oneforboth_further_plain_kernel(
         l6 = load_list("l6", offs6)
         load_plane(nc.sync, xo_s, xo_scales)
         nc.sync.dma_start(out=levels[1][:], in_=ta_rows[1])
-        nc.sync.dma_start(out=levels[2][:], in_=ta_rows[2])
-        l5 = load_list("l5", offs5)
-        nc.sync.dma_start(out=levels[3][:], in_=ta_rows[3])
         l4 = load_list("l4", offs4)
+        nc.sync.dma_start(out=levels[2][:], in_=ta_rows[2])
+        nc.sync.dma_start(out=levels[3][:], in_=ta_rows[3])
+        l5 = load_list("l5", offs5)
         ws_w = load_words(nc.sync, "ws_w", ws_words[0].rearrange("p c r -> p (c r)"), N, U32)
         wb_w = load_words(nc.sync, "wb_w", wb_words[0], N, U16)
         load_plane(nc.sync, ws_s, ws_scales)
@@ -167,12 +167,15 @@ def tile_list_fadedread_oneforboth_further_plain_kernel(
             nc.scalar.copy(both[t][:], ab_ps[t])
         for t in range(early, PACK):
             put(t)
-        for t in range(PACK):
+        board_pick = [new("board_pick%d" % t, [P, O], F32) for t in range(early)]
+        for t in range(early):
+            pick(t)
+            nc.vector.tensor_copy(board_pick[t][:], board[t][:].indirect(l4[:]))
+            nc.gpsimd.tensor_tensor(diff[:, t, :], board_pick[t][:], b_pick[t][:], ALU.subtract)
+        for t in range(early, PACK):
             pick(t)
         look(1)
         look(2)
-        subtract(0)
-        subtract(1)
         magnitude(slice(0, 2))
         look(3)
         subtract(2)

from contextlib import ExitStack

import concourse.mybir as mybir

K, T, Z, J, R, C, O, Q, N = 512, 1024, 1024, 256, 512, 512, 256, 1024, 256
FLOPS = 2 * (2 * K * R * J + R * N * O + K * N * O)

F32 = mybir.dt.float32
BF16 = mybir.dt.bfloat16
I32 = mybir.dt.int32
U32 = mybir.dt.uint32
U16 = mybir.dt.uint16
U8 = mybir.dt.uint8
E4M3 = mybir.dt.float8_e4m3fn_x4
E5M2 = mybir.dt.float8_e5m2_x4
E2M1 = mybir.dt.float4_e2m1fn_x4
ALU = mybir.AluOpType
ACT = mybir.ActivationFunctionType
AX = mybir.AxisListType
P = 128
PACK = 4


def tile_list_fadedread_oneforboth_further_plain_kernel(
    tc, xt_words, xt_scales, xo_words, xo_scales, w_words, w_scales, ta, wb_words, wb_scales,
    ws_words, ws_scales, offs, offs2, offs3, offs4, offs5, offs6, offs7, out,
):
    nc = tc.nc
    with ExitStack() as ctx:
        lists = ctx.enter_context(tc.tile_pool(name="lists", bufs=1))
        sb = ctx.enter_context(tc.tile_pool(name="sb", bufs=1))
        ps = ctx.enter_context(tc.psum_pool(name="ps", bufs=1))

        def new(name, shape, dtype):
            return sb.tile(shape, dtype, name=name, align_bytes=64)

        def load_list(name, src):
            tile = lists.tile([P, J // 16], U16, name=name)
            nc.sync.dma_start(tile[:], src)
            return tile

        def zeroed_plane(name, width):
            tile = new(name, [P, width], U8)
            nc.vector.memset(tile[:].bitcast(I32), 0)
            return tile

        def load_plane(queue, tile, src):
            for quad in range(4):
                queue.dma_start(out=tile[32 * quad : 32 * quad + 4, :].bitcast(I32),
                                in_=src[0, 4 * quad : 4 * quad + 4, :].bitcast(I32))

        def load_words(queue, name, src, width, dtype):
            tile = new(name, [P, width], dtype)
            queue.dma_start(out=tile[:].bitcast(I32), in_=src.bitcast(I32))
            return tile

        def gather(name, window, offsets, dtype):
            tile = new(name, [P, J], dtype)
            nc.vector.tensor_copy(tile[:], window[:].indirect(offsets[:]))
            return tile

        xt_s = zeroed_plane("xt_s", T)
        w_s = zeroed_plane("w_s", R)
        xo_s = zeroed_plane("xo_s", Z)
        ws_s = zeroed_plane("ws_s", N)
        wb_s = zeroed_plane("wb_s", N)
        board = [new("board%d" % t, [P, C], F32) for t in range(PACK)]
        for t in range(PACK):
            nc.vector.memset(board[t][:], 0.0)

        ta_rows = ta.rearrange("(p t) q -> t p q", t=PACK)
        levels = [new("levels%d" % t, [P, Q], F32) for t in range(PACK)]
        xt_w = load_words(nc.scalar, "xt_w", xt_words[0], T, U16)
        l1 = load_list("l1", offs)
        load_plane(nc.sync, xt_s, xt_scales)
        w_w = load_words(nc.sync, "w_w", w_words[0].rearrange("p c r -> p (c r)"), R, U32)
        xo_w = load_words(nc.sync, "xo_w", xo_words[0].rearrange("p c r -> p (c r)"), Z, U32)
        load_plane(nc.sync, w_s, w_scales)
        l7 = load_list("l7", offs7)
        l2 = load_list("l2", offs2)
        nc.sync.dma_start(out=levels[0][:], in_=ta_rows[0])
        l3 = load_list("l3", offs3)
        l6 = load_list("l6", offs6)
        load_plane(nc.sync, xo_s, xo_scales)
        nc.sync.dma_start(out=levels[1][:], in_=ta_rows[1])
        l4 = load_list("l4", offs4)
        nc.sync.dma_start(out=levels[2][:], in_=ta_rows[2])
        nc.sync.dma_start(out=levels[3][:], in_=ta_rows[3])
        l5 = load_list("l5", offs5)
        ws_w = load_words(nc.sync, "ws_w", ws_words[0].rearrange("p c r -> p (c r)"), N, U32)
        wb_w = load_words(nc.sync, "wb_w", wb_words[0], N, U16)
        load_plane(nc.sync, ws_s, ws_scales)
        load_plane(nc.sync, wb_s, wb_scales)

        xa_w = gather("xa_w", xt_w, l1, U16)
        xa_s = gather("xa_s", xt_s, l1, U8)
        wp_w = new("wp_w", [P, R], U32)
        wp_s = new("wp_s", [P, R], U8)
        nc.vector.tensor_copy(wp_w[:].rearrange("p (t m) -> p m t", t=PACK), w_w[:].rearrange("p (m t) -> p m t", t=PACK))
        nc.vector.tensor_copy(wp_s[:].rearrange("p (t m) -> p t m", t=PACK), w_s[:].rearrange("p (m t) -> p t m", t=PACK))

        both = [new("both%d" % t, [P, 2 * J], F32) for t in range(PACK)]
        early = 2
        a_ps, b_ps, ab_ps = [], [], []
        for t in range(PACK):
            if t < early:
                a_ps.append(ps.tile([P, J], F32, name="a_ps%d" % t, tag="bank%d" % t)[:])
                b_ps.append(ps.tile([P, J], F32, name="b_ps%d" % t)[:])
                ab_ps.append(None)
            else:
                bank = ps.tile([P, 2 * J], F32, name="ab_ps%d" % t)
                a_ps.append(bank[:, J:])
                b_ps.append(bank[:, :J])
                ab_ps.append(bank[:])
        for t in range(PACK):
            cols = slice(t * P, (t + 1) * P)
            nc.tensor.matmul_mx(out=a_ps[t], lhsT=wp_w[:, cols].bitcast(E4M3), lhsT_scale=wp_s[:, cols],
                                rhs=xa_w[:].bitcast(E2M1), rhs_scale=xa_s[:], start=True, stop=True)

        half = O // 2
        neg_top = [new("neg_top%d" % t, [P, 1], F32) for t in range(PACK)]
        fade = new("fade", [P, PACK, O], F32)
        b_pick = [new("b_pick%d" % t, [P, O], F32) for t in range(PACK)]
        diff = new("diff", [P, PACK, O], F32)
        size = new("size", [P, PACK, half], F32)
        signed = new("signed", [P, PACK, half], F32)

        xs_w = gather("xs_w", xt_w, l7, U16)
        xs_s = gather("xs_s", xt_s, l7, U8)
        xb_w = gather("xb_w", xo_w, l2, U32)
        xb_s = gather("xb_s", xo_s, l2, U8)
        for t in range(PACK):
            cols = slice(t * P, (t + 1) * P)
            nc.tensor.matmul_mx(out=b_ps[t], lhsT=wp_w[:, cols].bitcast(E4M3), lhsT_scale=wp_s[:, cols],
                                rhs=xb_w[:].bitcast(E4M3), rhs_scale=xb_s[:], start=True, stop=True)

        def top(t):
            nc.vector.tensor_reduce(neg_top[t][:], levels[t][:], axis=AX.X, op=ALU.max, negate=True)

        def put(t):
            nc.scalar.activation(board[t][:].indirect(l3[:]), both[t][:, J:], ACT.Copy)

        def look(t):
            nc.scalar.activation(fade[:, t, :], levels[t][:].indirect(l6[:]), ACT.Exp, bias=neg_top[t][:])

        def pick(t):
            nc.vector.tensor_copy(b_pick[t][:], both[t][:].indirect(l5[:]))

        def subtract(t):
            nc.vector.tensor_tensor(diff[:, t, :], board[t][:].indirect(l4[:]), b_pick[t][:], ALU.subtract)

        def magnitude(planes):
            nc.scalar.activation(size[:, planes, :], diff[:, planes, :half], ACT.Abs)

        def weigh(planes):
            nc.vector.tensor_tensor(signed[:, planes, :], diff[:, planes, half:], fade[:, planes, half:], ALU.mult)

        for t in range(PACK):
            top(t)
        for t in range(early):
            nc.scalar.copy(both[t][:, J:], a_ps[t])
            put(t)
        look(0)
        for t in range(early):
            nc.scalar.copy(both[t][:, :J], b_ps[t])
        for t in range(early, PACK):
            nc.scalar.copy(both[t][:], ab_ps[t])
        for t in range(early, PACK):
            put(t)
        board_pick = [new("board_pick%d" % t, [P, O], F32) for t in range(early)]
        for t in range(early):
            pick(t)
            nc.vector.tensor_copy(board_pick[t][:], board[t][:].indirect(l4[:]))
            nc.gpsimd.tensor_tensor(diff[:, t, :], board_pick[t][:], b_pick[t][:], ALU.subtract)
        for t in range(early, PACK):
            pick(t)
        look(1)
        look(2)
        magnitude(slice(0, 2))
        look(3)
        subtract(2)
        subtract(3)
        magnitude(slice(2, 4))
        weigh(slice(0, 3))
        weigh(slice(3, 4))

        y_lo = ps.tile([P, 2, half], F32, name="y_lo", tag="bank0")
        y_hi = [ps.tile([P, half], F32, name="y_hi%d" % h) for h in range(2)]
        y_ps = [[y_lo[:, 0, :], y_lo[:, 1, :]], [y_hi[0][:], y_hi[1][:]]]
        for u in range(2):
            places = slice(u * half, (u + 1) * half)
            for h in range(2):
                cols = slice(h * P, (h + 1) * P)
                nc.tensor.matmul_mx(out=y_ps[u][h], lhsT=ws_w[:, cols].bitcast(E4M3), lhsT_scale=ws_s[:, cols],
                                    rhs=xs_w[:, places].bitcast(E2M1), rhs_scale=xs_s[:, places],
                                    start=(u == 1 or h == 0), stop=False)

        hid = [new("hid%d" % u, [P, PACK * half], BF16) for u in range(2)]
        nc.vector.tensor_tensor(hid[0][:].rearrange("p (c i t) -> p c t i", i=4, t=PACK),
                                size[:].rearrange("p t (c i) -> p c t i", i=4),
                                fade[:, :, :half].rearrange("p t (c i) -> p c t i", i=4), ALU.mult)
        nc.scalar.activation(hid[1][:].rearrange("p (c i t) -> p c t i", i=4, t=PACK),
                             signed[:].rearrange("p t (c i) -> p c t i", i=4), ACT.Abs)
        for u in range(2):
            hid_w = new("hid_w%d" % u, [P, half], U32)
            hid_s = new("hid_s%d" % u, [P, half], U8)
            nc.vector.quantize_mx(out=hid_w[:].bitcast(E5M2), scales=hid_s[:], in_=hid[u][:])
            for h in range(2):
                cols = slice(h * P, (h + 1) * P)
                nc.tensor.matmul_mx(out=y_ps[u][h], lhsT=wb_w[:, cols].bitcast(E2M1), lhsT_scale=wb_s[:, cols],
                                    rhs=hid_w[:].bitcast(E5M2), rhs_scale=hid_s[:],
                                    start=False, stop=(u == 1 or h == 1))
        out_rows = out.rearrange("(h p) o -> p h o", h=2)
        y_a = new("y_a", [P, 2, half], F32)
        nc.vector.tensor_copy(y_a[:], y_lo[:])
        nc.sync.dma_start(out=out_rows[:, :, :half], in_=y_a[:])
        y_b = [new("y_b%d" % h, [P, half], F32) for h in range(2)]
        nc.scalar.copy(y_b[0][:], y_hi[0][:])
        nc.scalar.dma_start(out=out_rows[:, 0, half:], in_=y_b[0][:])
        nc.vector.tensor_copy(y_b[1][:], y_hi[1][:])
        nc.sync.dma_start(out=out_rows[:, 1, half:], in_=y_b[1][:])
